import numpy as np
import ml_dtypes


def mxq(x, axis, fmt="e4m3"):
    dtype, down = {"e4m3": (ml_dtypes.float8_e4m3fn, 7), "e5m2": (ml_dtypes.float8_e5m2, 14)}[fmt]
    v = np.moveaxis(np.asarray(x, np.float32).astype(ml_dtypes.bfloat16).astype(np.float64), axis, -1)
    blocks = v.reshape(v.shape[:-1] + (-1, 32))
    amax = np.abs(blocks).max(-1, keepdims=True)
    byte = np.maximum(np.where(amax > 0, np.frexp(amax)[1] - 1 + 127, 0) - down, 1)
    scale = np.exp2(byte - 127.0)
    codes = (blocks / scale).astype(np.float32).astype(dtype).astype(np.float64)
    return np.moveaxis((codes * scale).reshape(v.shape), -1, axis)


WIDE = False


def mx_kscale(k):
    if not WIDE:
        return np.ones(k)
    levels = np.array([10, -10, 5, -5, 0])
    if k % 512:
        return np.exp2(np.random.permutation(np.resize(levels, k // 32))).repeat(32)
    a = np.empty((k // 512, 16))
    for p in range(k // 512):
        a[p, :8] = np.random.permutation(np.resize(levels, 8))
        for g in range(8):
            far = levels[np.abs(levels - a[p, g]) >= 10]
            a[p, g + 8] = far[np.random.randint(len(far))]
    return np.exp2(a.ravel()).repeat(32)


def f64(x):
    return np.asarray(x).astype(np.float64)


def striped(idx):
    return np.tile(idx.reshape(-1, 16).T, (8, 1)).astype(np.uint16)


def unstriped(offs):
    return offs[:16].T.reshape(-1).astype(np.int64)


def striped8(idx):
    return np.concatenate([x.reshape(-1, 16).T for x in idx]).astype(np.uint16)


def runs(offs, k):
    lists = np.stack([offs[16 * r : 16 * r + 16].T.reshape(-1) for r in range(8)]).astype(np.int64)
    return lists[np.arange(k) % 512 // 64]


def pack_weight(w):
    k, n = w.shape
    w = f64(np.asarray(w, np.float32).astype(ml_dtypes.bfloat16)).reshape(k // 32, 32, n)
    amax = np.abs(w).max(1)
    byte = np.clip(np.where(amax > 0, np.frexp(amax)[1] - 1 + 127 - 7, 1), 1, 254)
    scaled = (w * np.exp2(127.0 - byte)[:, None, :]).reshape(k, n).astype(np.float32)
    words = np.ascontiguousarray(scaled.reshape(k // 512, 128, 4, n).transpose(0, 1, 3, 2)).astype(ml_dtypes.float8_e4m3fn).view(np.uint8)
    return words, np.ascontiguousarray(byte.astype(np.uint8).reshape(k // 512, 16, n))


def unpack_weight(words, scales):
    g, p, n, _ = words.shape
    vals = np.ascontiguousarray(words).view(ml_dtypes.float8_e4m3fn).astype(np.float64) * np.repeat(np.exp2(scales.astype(np.float64) - 127.0), 8, axis=1)[..., None]
    return vals.transpose(0, 1, 3, 2).reshape(g * 512, n)

def planes(y):
    n, m = y.shape
    v = y.astype(np.float32).astype(ml_dtypes.bfloat16).astype(np.float64).reshape(n // 32, 32, m)
    top = np.abs(v).max(1)
    byte = np.clip(np.where(top > 0, np.frexp(top)[1] - 1 + 127 - 7, 1), 1, 254)
    codes = (v * np.exp2(127.0 - byte)[:, None, :]).reshape(n, m).astype(np.float32).astype(ml_dtypes.float8_e4m3fn).view(np.uint8)
    words = codes.reshape(n // 512, 128, 4, m).transpose(0, 1, 3, 2)
    return np.ascontiguousarray(words), np.ascontiguousarray(byte.astype(np.uint8).reshape(n // 512, 16, m))


K, T, S, N, H, G, W, U = 512, 1024, 512, 512, 512, 2048, 256, 384


def setup_inputs():
    n = np.random.standard_normal
    s = mx_kscale(K)[:, None]
    u = mx_kscale(S)
    packed_xT = pack_weight(n((K, T)) * s)
    packed_w1 = pack_weight(n((K, H)) / np.sqrt(K) / s)
    packed_dT = pack_weight(n((K, G)) / s)
    packed_w2 = pack_weight(n((H, N)) / np.sqrt(2 * H) / u[:, None])
    packed_w3 = pack_weight(n((H, N)) / np.sqrt(2 * H) / u[:, None])
    perm = np.stack([np.random.permutation(S) for _ in range(8)])
    return {
        "x_words": packed_xT[0],
        "x_scales": packed_xT[1],
        "w1_words": packed_w1[0],
        "w1_scales": packed_w1[1],
        "d_words": packed_dT[0],
        "d_scales": packed_dT[1],
        "gn": (np.random.uniform(0.5, 1.5, (H, 1)) * u[:, None]).astype(np.float32),
        "gk": (np.random.uniform(0.5, 1.5, (H, 1)) * u[:, None]).astype(np.float32),
        "w2_words": packed_w2[0],
        "w2_scales": packed_w2[1],
        "w3_words": packed_w3[0],
        "w3_scales": packed_w3[1],
        "offs": striped(np.random.permutation(T)[:S]),
        "kidx": striped8(np.random.randint(0, G, (8, H))),
        "two": striped(np.random.permutation(T)[:S]),
        "n1": striped(np.random.permutation(S)),
        "n2": striped(np.random.permutation(S)),
        "n3": striped8(perm[:, :W]),
        "n4": striped8(perm[:, W:]),
        "n5": striped(np.random.permutation(S)[:U]),
        "n6": striped(np.random.permutation(S)[:U]),
    }


def reference(x_words, x_scales, w1_words, w1_scales, d_words, d_scales, gn, gk, w2_words, w2_scales, w3_words, w3_scales, offs, kidx, two, n1, n2, n3, n4, n5, n6):
    xq = unpack_weight(x_words, x_scales)[:, unstriped(offs)]
    y = unpack_weight(w1_words, w1_scales).T @ xq
    z = f64(gn) * (y * (y[:, unstriped(n1)] - y[:, unstriped(n2)]))
    d_kidx = unpack_weight(d_words, d_scales)[np.arange(K)[:, None], runs(kidx, K)]
    x_two = unpack_weight(x_words, x_scales)[:, unstriped(two)]
    s = 0.0625 * (d_kidx.T @ x_two)
    pa = s[np.arange(H)[:, None], runs(n3, H)]
    pb = s[np.arange(H)[:, None], runs(n4, H)]
    rb = np.maximum(0.5 * pa, pb)
    ra = pb - pa
    ds = np.zeros((H, S))
    ds[np.arange(H)[:, None], runs(n3, H)] = ra
    dt = ds.copy()
    dt[np.arange(H)[:, None], runs(n4, H)] = rb
    z2 = f64(gk) * dt
    h = unpack_weight(w2_words, w2_scales).T @ mxq(z, 0, "e4m3") + unpack_weight(w3_words, w3_scales).T @ mxq(z2, 0, "e4m3")
    pa2 = h[:, unstriped(n6)]
    old = h[:, unstriped(n5)]
    ra2 = np.minimum(pa2, old) - (0.5 * pa2)
    out = h.copy()
    out[:, unstriped(n5)] = ra2
    return (out,) + planes(out)

@@ -1,0 +1,256 @@
+from contextlib import ExitStack
+
+import concourse.mybir as mybir
+
+F32 = mybir.dt.float32
+BF16 = mybir.dt.bfloat16
+I32 = mybir.dt.int32
+U32 = mybir.dt.uint32
+U16 = mybir.dt.uint16
+U8 = mybir.dt.uint8
+FP8X4 = mybir.dt.float8_e4m3fn_x4
+COPY = mybir.ActivationFunctionType.Copy
+ADD = mybir.AluOpType.add
+SUB = mybir.AluOpType.subtract
+MULT = mybir.AluOpType.mult
+MAX = mybir.AluOpType.max
+MIN = mybir.AluOpType.min
+
+P = 128
+PACK = 4
+S = 512
+T = 1024
+G = 2048
+PAIRS = 256
+U = 384
+Y_WINDOW = 544
+H_WINDOW = 768
+V_COLS = 352
+FLOPS = 4 * 2 * 512 * 512 * 512
+
+
+def tile_picked_jkeywindliftkmin_none_po_kernel(
+    tc, x_words, x_scales, w1_words, w1_scales, d_words, d_scales, gn, gk, w2_words, w2_scales,
+    w3_words, w3_scales, offs, kidx, two, n1, n2, n3, n4, n5, n6, out_0, out_1, out_2
+):
+    nc = tc.nc
+    with ExitStack() as ctx:
+        keep = ctx.enter_context(tc.tile_pool(name="keep", bufs=1))
+        psum = ctx.enter_context(tc.psum_pool(name="psum", bufs=1))
+
+        def sb(shape, dtype, name):
+            return keep.tile(shape, dtype, name=name, align_bytes=64)
+
+        def load_list(src, name):
+            dst = keep.tile([P, src.shape[1]], U16, name=name)
+            nc.sync.dma_start(dst[:], src)
+            return dst
+
+        def load_words(src, name):
+            dst = sb([P, src.shape[2]], I32, name)
+            nc.sync.dma_start(dst[:], src[0].rearrange("p c r -> p (c r)").bitcast(I32))
+            return dst
+
+        def load_scale_rows(queues, dst, src, first):
+            for q in range(4):
+                queue = queues[q % len(queues)]
+                rows = slice(32 * q + first, 32 * q + first + 4)
+                queue.dma_start(dst[rows, :].bitcast(I32), src[0, 4 * q : 4 * q + 4, :].bitcast(I32))
+
+        def zeroed_bytes(width, name, engine):
+            dst = sb([P, width], U8, name)
+            engine.memset(dst[:].bitcast(I32), 0)
+            return dst
+
+        def dealt(src, dtype, name, engine=nc.vector):
+            dst = sb([P, S], dtype, name)
+            engine.tensor_copy(dst[:].rearrange("p (t m) -> p t m", t=PACK), src.rearrange("p (m t) -> p t m", t=PACK))
+            return dst
+
+        def picked(table, offsets, dtype, name):
+            dst = sb([P, S], dtype, name)
+            nc.vector.tensor_copy(dst[:], table.indirect(offsets[:]))
+            return dst
+
+        def product(bank, t, w_codes, w_plane, codes, plane, start, stop):
+            cols = slice(P * t, P * (t + 1))
+            nc.tensor.matmul_mx(out=bank[:], lhsT=w_codes[:, cols].bitcast(FP8X4), lhsT_scale=w_plane[:, cols],
+                                rhs=codes[:].bitcast(FP8X4), rhs_scale=plane[:], start=start, stop=stop)
+
+        def interleave(copy, dst, src, cols):
+            copy(dst[:, cols, :].rearrange("p (c i) t -> p c t i", i=4), src[:, :, cols].rearrange("p t (c i) -> p c t i", i=4))
+
+        def quantise(grouped, name):
+            codes = sb([P, S], U32, name + "_codes")
+            plane = sb([P, S], U8, name + "_plane")
+            nc.vector.quantize_mx(out=codes[:].bitcast(FP8X4), scales=plane[:], in_=grouped[:].rearrange("p c t -> p (c t)"))
+            return codes, plane
+
+        ds = zeroed_bytes(G, "ds", nc.gpsimd)
+        xs = zeroed_bytes(T, "xs", nc.vector)
+        w1s = zeroed_bytes(S, "w1s", nc.vector)
+        w23s = zeroed_bytes(S, "w23s", nc.vector)
+        kidx_t = load_list(kidx, "kidx_t")
+        nc.sync.dma_start(ds[0:P:8, :].bitcast(I32), d_scales[0].bitcast(I32))
+        xw = load_words(x_words, "xw")
+        two_t = load_list(two, "two_t")
+        load_scale_rows([nc.scalar], xs, x_scales, 0)
+        dw = load_words(d_words, "dw")
+        offs_t = load_list(offs, "offs_t")
+        w1w = load_words(w1_words, "w1w")
+        load_scale_rows([nc.scalar], w1s, w1_scales, 0)
+        n3_t = load_list(n3, "n3_t")
+        n4_t = load_list(n4, "n4_t")
+
+        y = [sb([P, Y_WINDOW], F32, f"y{t}") for t in range(PACK)]
+        h = [sb([P, H_WINDOW], F32, f"h{t}") for t in range(PACK)]
+        for t in range(PACK):
+            nc.gpsimd.memset(y[t][:, S:], 0.0)
+        for t in range(PACK):
+            nc.gpsimd.memset(h[t][:, S:], 0.0)
+
+        key_bytes = dealt(picked(ds[:], kidx_t, U8, "key_bytes_picked")[:], U8, "key_bytes")
+        key_plane = sb([P, S], U8, "key_plane")
+        for q in range(4):
+            nc.sync.dma_start(key_plane[32 * q : 32 * q + 4, :].bitcast(I32), key_bytes[32 * q : 32 * q + 32 : 8, :].bitcast(I32))
+        n1_t = load_list(n1, "n1_t")
+        n2_t = load_list(n2, "n2_t")
+        gn_t = sb([P, PACK], F32, "gn_t")
+        nc.sync.dma_start(gn_t[:], gn.rearrange("(p t) o -> p (t o)", t=PACK))
+        w2w = load_words(w2_words, "w2w")
+        w3w = load_words(w3_words, "w3w")
+        gk_t = sb([P, PACK], F32, "gk_t")
+        nc.sync.dma_start(gk_t[:], gk.rearrange("(p t) o -> p (t o)", t=PACK))
+        load_scale_rows([nc.sync], w23s, w2_scales, 0)
+        load_scale_rows([nc.sync], w23s, w3_scales, 4)
+        n5_t = load_list(n5, "n5_t")
+        n6_t = load_list(n6, "n6_t")
+
+        xt_plane = picked(xs[:], two_t, U8, "xt_plane")
+        xt_codes = picked(xw[:].bitcast(U32), two_t, U32, "xt_codes")
+        key_codes = dealt(picked(dw[:].bitcast(U32), kidx_t, U32, "key_codes_picked")[:], U32, "key_codes")
+        s_banks = [psum.tile([P, S], F32, name=f"bank_a{t}") for t in range(PACK)]
+        for t in range(PACK):
+            product(s_banks[t], t, key_codes, key_plane, xt_codes, xt_plane, True, True)
+
+        w1_codes = dealt(w1w[:].bitcast(U32), U32, "w1_codes", nc.gpsimd)
+        w1_plane = dealt(w1s[:], U8, "w1_plane", nc.gpsimd)
+        xq_plane = picked(xs[:], offs_t, U8, "dw")
+        xq_codes = picked(xw[:].bitcast(U32), offs_t, U32, "key_codes_picked")
+
+        z_rows = sb([P, PACK, S], BF16, "z_rows")
+
+        def make_z(t):
+            bank = psum.tile([P, S], F32, name=f"bank_a{t}")
+            product(bank, t, w1_codes, w1_plane, xq_codes, xq_plane, True, True)
+            nc.scalar.copy(y[t][:, :S], bank[:])
+            at_n1 = sb([P, S], F32, f"at_n1{t}")
+            at_n2 = sb([P, S], F32, f"at_n2{t}")
+            nc.scalar.activation(at_n1[:], y[t][:].indirect(n1_t[:]), COPY)
+            nc.scalar.activation(at_n2[:], y[t][:].indirect(n2_t[:]), COPY)
+            diff = sb([P, S], F32, f"diff{t}")
+            nc.vector.tensor_tensor(diff[:], at_n1[:], at_n2[:], SUB)
+            nc.vector.scalar_tensor_tensor(z_rows[:, t, :], diff[:], gn_t[:, t : t + 1], y[t][:, :S], MULT, MULT)
+
+        def pair_s(t):
+            s = sb([P, S], F32, f"s{t}")
+            nc.scalar.activation(s[:], s_banks[t][:], COPY, scale=0.0625)
+            neg_pa = sb([P, PAIRS], F32, f"neg_pa{t}")
+            pb = sb([P, PAIRS], F32, f"pb{t}")
+            nc.scalar.activation(neg_pa[:], s[:].indirect(n3_t[:]), COPY, scale=-1.0)
+            nc.scalar.activation(pb[:], s[:].indirect(n4_t[:]), COPY)
+            rb = sb([P, PAIRS], F32, f"rb{t}")
+            dt = sb([P, S], F32, f"dt{t}")
+            nc.vector.scalar_tensor_tensor(rb[:], neg_pa[:], -0.5, pb[:], MULT, MAX)
+            nc.vector.tensor_tensor(dt[:].indirect(n3_t[:]), pb[:], neg_pa[:], ADD)
+            nc.vector.tensor_copy(dt[:].indirect(n4_t[:]), rb[:])
+            return dt
+
+        def make_z2(t, dt):
+            nc.scalar.activation(z2_rows[:, t, :], dt[:], COPY, scale=gk_t[:, t : t + 1])
+
+        w2_codes = dealt(w2w[:].bitcast(U32), U32, "w2_codes", nc.gpsimd)
+        w3_codes = dealt(w3w[:].bitcast(U32), U32, "w3_codes", nc.gpsimd)
+        w23_plane = dealt(w23s[:], U8, "w23_plane", nc.gpsimd)
+        dts = [pair_s(0), pair_s(1)]
+        make_z(0)
+        make_z(1)
+        dts.append(pair_s(2))
+        make_z(2)
+        dts.append(pair_s(3))
+        z2_rows = sb([P, PACK, S], BF16, f"s{PACK - 1}")
+        nc.vector.tensor_scalar(z2_rows[:, PACK - 1, :], dts[PACK - 1][:], gk_t[:, PACK - 1 : PACK], None, MULT)
+        make_z(3)
+        for t in range(PACK - 1):
+            make_z2(t, dts[t])
+
+        z2_grouped = sb([P, S, PACK], BF16, "z2_grouped")
+        interleave(nc.scalar.copy, z2_grouped, z2_rows, slice(0, S))
+        z_grouped = sb([P, S, PACK], BF16, "z_grouped")
+        interleave(nc.vector.tensor_copy, z_grouped, z_rows, slice(0, S))
+        z_codes, z_plane = quantise(z_grouped, "z")
+        z2_codes, z2_plane = quantise(z2_grouped, "z2")
+        h_banks = [psum.tile([P, S], F32, name=f"bank_b{t}") for t in range(PACK)]
+        for t in range(PACK):
+            product(h_banks[t], t, w2_codes, w23_plane, z_codes, z_plane, True, False)
+        for t in range(PACK):
+            product(h_banks[t], t, w3_codes, w23_plane[4:], z2_codes, z2_plane, False, True)
+
+        out_rows = out_0.rearrange("(p t) j -> p t j", t=PACK)
+        o_rows = sb([P, PACK, S], BF16, "o_rows")
+        neg_half = [sb([P, U], F32, f"neg_half{t}") for t in range(PACK)]
+        old = [sb([P, U], F32, f"old{t}") for t in range(PACK)]
+        least = [sb([P, U], F32, f"least{t}") for t in range(PACK)]
+
+        def fetch_on_scalar(t):
+            nc.scalar.copy(h[t][:, :S], h_banks[t][:])
+            nc.scalar.activation(neg_half[t][:], h[t][:].indirect(n6_t[:]), COPY, scale=-0.5)
+            nc.scalar.activation(old[t][:], h[t][:].indirect(n5_t[:]), COPY)
+
+        def take_least(t):
+            nc.vector.scalar_tensor_tensor(least[t][:], neg_half[t][:], -2.0, old[t][:], MULT, MIN)
+
+        def put_on_vector(t):
+            nc.vector.tensor_tensor(h[t][:].indirect(n5_t[:]), least[t][:], neg_half[t][:], ADD)
+
+        def sum_for_scalar(t):
+            nc.vector.tensor_tensor(old[t][:], least[t][:], neg_half[t][:], ADD)
+
+        def put_on_scalar(t):
+            nc.scalar.activation(h[t][:].indirect(n5_t[:]), old[t][:], COPY)
+
+        def finish(t):
+            nc.sync.dma_start(out_rows[:, t, :], h[t][:, :S])
+            nc.vector.tensor_copy(o_rows[:, t, :], h[t][:, :S])
+
+        pa2 = sb([P, U], F32, "pa2")
+        nc.vector.tensor_copy(h[0][:, :S], h_banks[0][:])
+        nc.vector.tensor_copy(pa2[:], h[0][:].indirect(n6_t[:]))
+        nc.vector.tensor_copy(old[0][:], h[0][:].indirect(n5_t[:]))
+        nc.vector.tensor_scalar(neg_half[0][:], pa2[:], -0.5, None, MULT)
+        nc.vector.tensor_tensor(least[0][:], pa2[:], old[0][:], MIN)
+        fetch_on_scalar(2)
+        fetch_on_scalar(3)
+        fetch_on_scalar(1)
+        put_on_vector(0)
+        take_least(2)
+        sum_for_scalar(2)
+        finish(0)
+        take_least(3)
+        sum_for_scalar(3)
+        put_on_scalar(2)
+        take_least(1)
+        put_on_vector(1)
+        put_on_scalar(3)
+        finish(2)
+        finish(1)
+        finish(3)
+
+        o_grouped = sb([P, S, PACK], BF16, "o_grouped")
+        interleave(nc.vector.tensor_copy, o_grouped, o_rows, slice(0, V_COLS))
+        interleave(nc.scalar.copy, o_grouped, o_rows, slice(V_COLS, S))
+        o_codes, o_plane = quantise(o_grouped, "o")
+        nc.sync.dma_start(out_1[0].rearrange("p c r -> p (c r)").bitcast(I32), o_codes[:].bitcast(I32))
+        for q in range(4):
+            queue = nc.scalar if q % 2 == 0 else nc.sync
+            queue.dma_start(out_2[0, 4 * q : 4 * q + 4, :].bitcast(I32), o_plane[32 * q : 32 * q + 4, :].bitcast(I32))

@@ -86,21 +86,26 @@ def tile_picked_jkeywindliftkmin_none_po_kernel(
             nc.vector.quantize_mx(out=codes[:].bitcast(FP8X4), scales=plane[:], in_=grouped[:].rearrange("p c t -> p (c t)"))
             return codes, plane
 
-        ds = zeroed_bytes(G, "ds", nc.gpsimd)
-        xs = zeroed_bytes(T, "xs", nc.vector)
+        xs = zeroed_bytes(T, "xs", nc.gpsimd)
         w1s = zeroed_bytes(S, "w1s", nc.vector)
+        ds = zeroed_bytes(G, "ds", nc.vector)
         w23s = zeroed_bytes(S, "w23s", nc.vector)
-        kidx_t = load_list(kidx, "kidx_t")
-        nc.sync.dma_start(ds[0:P:8, :].bitcast(I32), d_scales[0].bitcast(I32))
-        xw = load_words(x_words, "xw")
-        two_t = load_list(two, "two_t")
-        load_scale_rows([nc.scalar], xs, x_scales, 0)
-        dw = load_words(d_words, "dw")
         offs_t = load_list(offs, "offs_t")
         w1w = load_words(w1_words, "w1w")
-        load_scale_rows([nc.scalar], w1s, w1_scales, 0)
+        xw = load_words(x_words, "xw")
+        load_scale_rows([nc.scalar, nc.sync], xs, x_scales, 0)
+        load_scale_rows([nc.scalar, nc.sync], w1s, w1_scales, 0)
+        kidx_t = load_list(kidx, "kidx_t")
+        nc.sync.dma_start(ds[0:P:8, :].bitcast(I32), d_scales[0].bitcast(I32))
+        two_t = load_list(two, "two_t")
+        n1_t = load_list(n1, "n1_t")
+        n2_t = load_list(n2, "n2_t")
+        dw = load_words(d_words, "dw")
         n3_t = load_list(n3, "n3_t")
         n4_t = load_list(n4, "n4_t")
+        w23w = sb([P, 2, S], I32, "w23w")
+        for a, src in enumerate((w2_words, w3_words)):
+            nc.sync.dma_start(w23w[:, a, :], src[0].rearrange("p c r -> p (c r)").bitcast(I32))
 
         y = [sb([P, Y_WINDOW], F32, f"y{t}") for t in range(PACK)]
         h = [sb([P, H_WINDOW], F32, f"h{t}") for t in range(PACK)]
@@ -109,23 +114,30 @@ def tile_picked_jkeywindliftkmin_none_po_kernel(
         for t in range(PACK):
             nc.gpsimd.memset(h[t][:, S:], 0.0)
 
+        w1_codes = dealt(w1w[:].bitcast(U32), U32, "w1_codes")
+        xq_plane = picked(xs[:], offs_t, U8, "xq_plane")
+        xq_codes = picked(xw[:].bitcast(U32), offs_t, U32, "xq_codes")
+        w1_plane = dealt(w1s[:], U8, "w1_plane")
+
+        def y_product(t, tag):
+            bank = psum.tile([P, S], F32, name=tag)
+            product(bank, t, w1_codes, w1_plane, xq_codes, xq_plane, True, True)
+            return bank
+
+        y_first = [y_product(t, f"bank_b{t}") for t in range(2)]
+
         key_bytes = dealt(picked(ds[:], kidx_t, U8, "key_bytes_picked")[:], U8, "key_bytes")
         key_plane = sb([P, S], U8, "key_plane")
         for q in range(4):
             nc.sync.dma_start(key_plane[32 * q : 32 * q + 4, :].bitcast(I32), key_bytes[32 * q : 32 * q + 32 : 8, :].bitcast(I32))
-        n1_t = load_list(n1, "n1_t")
-        n2_t = load_list(n2, "n2_t")
         gn_t = sb([P, PACK], F32, "gn_t")
         nc.sync.dma_start(gn_t[:], gn.rearrange("(p t) o -> p (t o)", t=PACK))
-        w2w = load_words(w2_words, "w2w")
-        w3w = load_words(w3_words, "w3w")
-        gk_t = sb([P, PACK], F32, "gk_t")
-        nc.sync.dma_start(gk_t[:], gk.rearrange("(p t) o -> p (t o)", t=PACK))
         load_scale_rows([nc.sync], w23s, w2_scales, 0)
         load_scale_rows([nc.sync], w23s, w3_scales, 4)
+        gk_t = sb([P, PACK], F32, "gk_t")
+        nc.sync.dma_start(gk_t[:], gk.rearrange("(p t) o -> p (t o)", t=PACK))
         n5_t = load_list(n5, "n5_t")
         n6_t = load_list(n6, "n6_t")
-
         xt_plane = picked(xs[:], two_t, U8, "xt_plane")
         xt_codes = picked(xw[:].bitcast(U32), two_t, U32, "xt_codes")
         key_codes = dealt(picked(dw[:].bitcast(U32), kidx_t, U32, "key_codes_picked")[:], U32, "key_codes")
@@ -133,68 +145,82 @@ def tile_picked_jkeywindliftkmin_none_po_kernel(
         for t in range(PACK):
             product(s_banks[t], t, key_codes, key_plane, xt_codes, xt_plane, True, True)
 
-        w1_codes = dealt(w1w[:].bitcast(U32), U32, "w1_codes", nc.gpsimd)
-        w1_plane = dealt(w1s[:], U8, "w1_plane", nc.gpsimd)
-        xq_plane = picked(xs[:], offs_t, U8, "dw")
-        xq_codes = picked(xw[:].bitcast(U32), offs_t, U32, "key_codes_picked")
-
         z_rows = sb([P, PACK, S], BF16, "z_rows")
 
-        def make_z(t):
-            bank = psum.tile([P, S], F32, name=f"bank_a{t}")
-            product(bank, t, w1_codes, w1_plane, xq_codes, xq_plane, True, True)
+        def fetch_y(t, bank, at_n1, at_n2):
             nc.scalar.copy(y[t][:, :S], bank[:])
-            at_n1 = sb([P, S], F32, f"at_n1{t}")
-            at_n2 = sb([P, S], F32, f"at_n2{t}")
-            nc.scalar.activation(at_n1[:], y[t][:].indirect(n1_t[:]), COPY)
-            nc.scalar.activation(at_n2[:], y[t][:].indirect(n2_t[:]), COPY)
-            diff = sb([P, S], F32, f"diff{t}")
-            nc.vector.tensor_tensor(diff[:], at_n1[:], at_n2[:], SUB)
-            nc.vector.scalar_tensor_tensor(z_rows[:, t, :], diff[:], gn_t[:, t : t + 1], y[t][:, :S], MULT, MULT)
+            nc.scalar.activation(at_n1, y[t][:].indirect(n1_t[:]), COPY)
+            nc.scalar.activation(at_n2, y[t][:].indirect(n2_t[:]), COPY)
 
-        def pair_s(t):
-            s = sb([P, S], F32, f"s{t}")
-            nc.scalar.activation(s[:], s_banks[t][:], COPY, scale=0.0625)
-            neg_pa = sb([P, PAIRS], F32, f"neg_pa{t}")
-            pb = sb([P, PAIRS], F32, f"pb{t}")
-            nc.scalar.activation(neg_pa[:], s[:].indirect(n3_t[:]), COPY, scale=-1.0)
-            nc.scalar.activation(pb[:], s[:].indirect(n4_t[:]), COPY)
-            rb = sb([P, PAIRS], F32, f"rb{t}")
-            dt = sb([P, S], F32, f"dt{t}")
+        def scale_z(t, bank, diff):
+            nc.vector.scalar_tensor_tensor(z_rows[:, t, :], diff, gn_t[:, t : t + 1], bank[:], MULT, MULT)
+
+        def pair_s(first, tags):
+            neg_pa = sb([P, 2, PAIRS], F32, f"neg_pa{first}")
+            pb = sb([P, 2, PAIRS], F32, f"pb{first}")
+            rb = sb([P, 2, PAIRS], F32, f"rb{first}")
+            dt = [sb([P, S], F32, f"dt{first + a}") for a in range(2)]
+            for a in range(2):
+                s = sb([P, S], F32, tags[a])
+                nc.scalar.activation(s[:], s_banks[first + a][:], COPY, scale=0.0625)
+                nc.scalar.activation(neg_pa[:, a, :], s[:].indirect(n3_t[:]), COPY, scale=-1.0)
+                nc.scalar.activation(pb[:, a, :], s[:].indirect(n4_t[:]), COPY)
+                nc.vector.tensor_tensor(dt[a][:].indirect(n3_t[:]), pb[:, a, :], neg_pa[:, a, :], ADD)
             nc.vector.scalar_tensor_tensor(rb[:], neg_pa[:], -0.5, pb[:], MULT, MAX)
-            nc.vector.tensor_tensor(dt[:].indirect(n3_t[:]), pb[:], neg_pa[:], ADD)
-            nc.vector.tensor_copy(dt[:].indirect(n4_t[:]), rb[:])
+            for a in range(2):
+                nc.vector.tensor_copy(dt[a][:].indirect(n4_t[:]), rb[:, a, :])
             return dt
 
-        def make_z2(t, dt):
-            nc.scalar.activation(z2_rows[:, t, :], dt[:], COPY, scale=gk_t[:, t : t + 1])
+        at_n1 = [sb([P, S], F32, f"at_n1{t}") for t in range(2)]
+        at_n2 = [sb([P, S], F32, f"at_n2{t}") for t in range(2)]
+        fetch_y(0, y_first[0], at_n1[0][:], at_n2[0][:])
+        diff0 = sb([P, S], F32, "key_codes_picked")
+        nc.vector.tensor_tensor(diff0[:], at_n1[0][:], at_n2[0][:], SUB)
+        w23_codes = sb([P, 2, S], I32, "dw")
+        nc.vector.tensor_copy(w23_codes[:].rearrange("p a (t m) -> p a t m", t=PACK), w23w[:].rearrange("p a (m t) -> p a t m", t=PACK))
+        w2_codes = w23_codes[:, 0, :]
+        w3_codes = w23_codes[:, 1, :]
+        scale_z(0, y_first[0], diff0[:])
+        fetch_y(1, y_first[1], at_n1[1][:], at_n2[1][:])
+        diff1 = sb([P, S], F32, "at_n10")
+        nc.vector.tensor_tensor(diff1[:], at_n1[1][:], at_n2[1][:], SUB)
+        scale_z(1, y_first[1], diff1[:])
+        dts = pair_s(0, ["s0", "s1"])
 
-        w2_codes = dealt(w2w[:].bitcast(U32), U32, "w2_codes", nc.gpsimd)
-        w3_codes = dealt(w3w[:].bitcast(U32), U32, "w3_codes", nc.gpsimd)
-        w23_plane = dealt(w23s[:], U8, "w23_plane", nc.gpsimd)
-        dts = [pair_s(0), pair_s(1)]
-        make_z(0)
-        make_z(1)
-        dts.append(pair_s(2))
-        make_z(2)
-        dts.append(pair_s(3))
-        z2_rows = sb([P, PACK, S], BF16, f"s{PACK - 1}")
-        nc.vector.tensor_scalar(z2_rows[:, PACK - 1, :], dts[PACK - 1][:], gk_t[:, PACK - 1 : PACK], None, MULT)
-        make_z(3)
-        for t in range(PACK - 1):
-            make_z2(t, dts[t])
+        late_n1 = sb([P, 2, S], F32, "late_n1")
+        late_n2 = sb([P, 2, S], F32, "late_n2")
+        late_diff = sb([P, 2, S], F32, "late_diff")
+        y_late = [y_product(2 + a, f"bank_a{1 - a}") for a in range(2)]
+        for a in range(2):
+            fetch_y(2 + a, y_late[a], late_n1[:, a, :], late_n2[:, a, :])
+        w23_plane = dealt(w23s[:], U8, "pb0")
+        nc.vector.tensor_tensor(late_diff[:], late_n1[:], late_n2[:], SUB)
+        for a in range(2):
+            scale_z(2 + a, y_late[a], late_diff[:, a, :])
+        dts = dts + pair_s(2, ["y3", "y2"])
 
-        z2_grouped = sb([P, S, PACK], BF16, "z2_grouped")
-        interleave(nc.scalar.copy, z2_grouped, z2_rows, slice(0, S))
+        z2_rows = sb([P, PACK, S], BF16, "y2")
+        for t in range(2):
+            nc.scalar.activation(z2_rows[:, t, :], dts[t][:], COPY, scale=gk_t[:, t : t + 1])
         z_grouped = sb([P, S, PACK], BF16, "z_grouped")
-        interleave(nc.vector.tensor_copy, z_grouped, z_rows, slice(0, S))
+        interleave(nc.scalar.copy, z_grouped, z_rows, slice(0, S))
         z_codes, z_plane = quantise(z_grouped, "z")
+        nc.scalar.activation(z2_rows[:, 2, :], dts[2][:], COPY, scale=gk_t[:, 2:3])
+        nc.vector.tensor_scalar(z2_rows[:, 3, :], dts[3][:], gk_t[:, 3:4], None, MULT)
+        z2_grouped = sb([P, S, PACK], BF16, "z2_grouped")
+        interleave(nc.vector.tensor_copy, z2_grouped, z2_rows, slice(0, V_COLS))
+        interleave(nc.scalar.copy, z2_grouped, z2_rows, slice(V_COLS, S))
         z2_codes, z2_plane = quantise(z2_grouped, "z2")
         h_banks = [psum.tile([P, S], F32, name=f"bank_b{t}") for t in range(PACK)]
-        for t in range(PACK):
-            product(h_banks[t], t, w2_codes, w23_plane, z_codes, z_plane, True, False)
-        for t in range(PACK):
-            product(h_banks[t], t, w3_codes, w23_plane[4:], z2_codes, z2_plane, False, True)
+        with_z = (w2_codes, w23_plane, z_codes, z_plane)
+        with_z2 = (w3_codes, w23_plane[4:], z2_codes, z2_plane)
+        for t in range(2):
+            product(h_banks[t], t, *with_z, True, False)
+        for t in range(2):
+            product(h_banks[t], t, *with_z2, False, True)
+        for t in range(2, PACK):
+            product(h_banks[t], t, *with_z2, True, False)
+            product(h_banks[t], t, *with_z, False, True)
 
         out_rows = out_0.rearrange("(p t) j -> p t j", t=PACK)
         o_rows = sb([P, PACK, S], BF16, "o_rows")
@@ -229,22 +255,22 @@ def tile_picked_jkeywindliftkmin_none_po_kernel(
         nc.vector.tensor_copy(old[0][:], h[0][:].indirect(n5_t[:]))
         nc.vector.tensor_scalar(neg_half[0][:], pa2[:], -0.5, None, MULT)
         nc.vector.tensor_tensor(least[0][:], pa2[:], old[0][:], MIN)
+        fetch_on_scalar(1)
         fetch_on_scalar(2)
         fetch_on_scalar(3)
-        fetch_on_scalar(1)
         put_on_vector(0)
+        take_least(1)
+        sum_for_scalar(1)
+        finish(0)
         take_least(2)
         sum_for_scalar(2)
-        finish(0)
+        put_on_scalar(1)
         take_least(3)
-        sum_for_scalar(3)
+        put_on_vector(3)
         put_on_scalar(2)
-        take_least(1)
-        put_on_vector(1)
-        put_on_scalar(3)
-        finish(2)
         finish(1)
         finish(3)
+        finish(2)
 
         o_grouped = sb([P, S, PACK], BF16, "o_grouped")
         interleave(nc.vector.tensor_copy, o_grouped, o_rows, slice(0, V_COLS))

@@ -87,12 +87,12 @@ def tile_picked_jkeywindliftkmin_none_po_kernel(
             return codes, plane
 
         xs = zeroed_bytes(T, "xs", nc.gpsimd)
-        w1s = zeroed_bytes(S, "w1s", nc.vector)
+        w1s = zeroed_bytes(S, "w1s", nc.gpsimd)
         ds = zeroed_bytes(G, "ds", nc.vector)
         w23s = zeroed_bytes(S, "w23s", nc.vector)
         offs_t = load_list(offs, "offs_t")
-        w1w = load_words(w1_words, "w1w")
         xw = load_words(x_words, "xw")
+        w1w = load_words(w1_words, "w1w")
         load_scale_rows([nc.scalar, nc.sync], xs, x_scales, 0)
         load_scale_rows([nc.scalar, nc.sync], w1s, w1_scales, 0)
         kidx_t = load_list(kidx, "kidx_t")
@@ -114,9 +114,9 @@ def tile_picked_jkeywindliftkmin_none_po_kernel(
         for t in range(PACK):
             nc.gpsimd.memset(h[t][:, S:], 0.0)
 
-        w1_codes = dealt(w1w[:].bitcast(U32), U32, "w1_codes")
-        xq_plane = picked(xs[:], offs_t, U8, "xq_plane")
+        w1_codes = dealt(w1w[:].bitcast(U32), U32, "w1_codes", nc.gpsimd)
         xq_codes = picked(xw[:].bitcast(U32), offs_t, U32, "xq_codes")
+        xq_plane = picked(xs[:], offs_t, U8, "xq_plane")
         w1_plane = dealt(w1s[:], U8, "w1_plane")
 
         def y_product(t, tag):
@@ -187,30 +187,48 @@ def tile_picked_jkeywindliftkmin_none_po_kernel(
         scale_z(1, y_first[1], diff1[:])
         dts = pair_s(0, ["s0", "s1"])
 
-        late_n1 = sb([P, 2, S], F32, "late_n1")
-        late_n2 = sb([P, 2, S], F32, "late_n2")
-        late_diff = sb([P, 2, S], F32, "late_diff")
-        y_late = [y_product(2 + a, f"bank_a{1 - a}") for a in range(2)]
-        for a in range(2):
-            fetch_y(2 + a, y_late[a], late_n1[:, a, :], late_n2[:, a, :])
-        w23_plane = dealt(w23s[:], U8, "pb0")
-        nc.vector.tensor_tensor(late_diff[:], late_n1[:], late_n2[:], SUB)
-        for a in range(2):
-            scale_z(2 + a, y_late[a], late_diff[:, a, :])
-        dts = dts + pair_s(2, ["y3", "y2"])
+        def late_z(t, bank):
+            late_n1 = sb([P, S], F32, f"at_n1{t}")
+            late_n2 = sb([P, S], F32, f"at_n2{t}")
+            fetch_y(t, bank, late_n1[:], late_n2[:])
+            diff = sb([P, S], F32, f"diff{t}")
+            nc.gpsimd.tensor_tensor(diff[:], late_n1[:], late_n2[:], SUB)
+            scale_z(t, bank, diff[:])
 
-        z2_rows = sb([P, PACK, S], BF16, "y2")
+        def fetch_s(t, tag):
+            s = sb([P, S], F32, tag)
+            neg_pa = sb([P, PAIRS], F32, f"neg_pa{t}")
+            pb = sb([P, PAIRS], F32, f"pb{t}")
+            dt = sb([P, S], F32, f"dt{t}")
+            nc.scalar.activation(s[:], s_banks[t][:], COPY, scale=0.0625)
+            nc.scalar.activation(neg_pa[:], s[:].indirect(n3_t[:]), COPY, scale=-1.0)
+            nc.scalar.activation(pb[:], s[:].indirect(n4_t[:]), COPY)
+            rb = sb([P, PAIRS], F32, f"rb{t}")
+            nc.vector.scalar_tensor_tensor(rb[:], neg_pa[:], -0.5, pb[:], MULT, MAX)
+            nc.vector.tensor_tensor(dt[:].indirect(n3_t[:]), pb[:], neg_pa[:], ADD)
+            nc.vector.tensor_copy(dt[:].indirect(n4_t[:]), rb[:])
+            return dt
+
+        w23_plane = dealt(w23s[:], U8, "pb0")
+        late_z(2, y_product(2, "bank_a1"))
+        dts.append(fetch_s(2, "y2"))
+        late_z(3, y_product(3, "bank_a2"))
+        dts.append(fetch_s(3, "y3"))
+
+        z2_rows = sb([P, PACK, S], BF16, "y3")
         for t in range(2):
             nc.scalar.activation(z2_rows[:, t, :], dts[t][:], COPY, scale=gk_t[:, t : t + 1])
         z_grouped = sb([P, S, PACK], BF16, "z_grouped")
         interleave(nc.scalar.copy, z_grouped, z_rows, slice(0, S))
-        z_codes, z_plane = quantise(z_grouped, "z")
         nc.scalar.activation(z2_rows[:, 2, :], dts[2][:], COPY, scale=gk_t[:, 2:3])
         nc.vector.tensor_scalar(z2_rows[:, 3, :], dts[3][:], gk_t[:, 3:4], None, MULT)
-        z2_grouped = sb([P, S, PACK], BF16, "z2_grouped")
-        interleave(nc.vector.tensor_copy, z2_grouped, z2_rows, slice(0, V_COLS))
-        interleave(nc.scalar.copy, z2_grouped, z2_rows, slice(V_COLS, S))
-        z2_codes, z2_plane = quantise(z2_grouped, "z2")
+        z_codes, z_plane = quantise(z_grouped, "z")
+        z2_codes = sb([P, S], U32, "z2_codes")
+        z2_plane = sb([P, S], U8, "z2_plane")
+        for copy, cols, tag in ((nc.vector.tensor_copy, slice(0, S // 2), "z_grouped"), (nc.scalar.copy, slice(S // 2, S), "z2_grouped")):
+            half = sb([P, S // 2, PACK], BF16, tag)
+            copy(half[:].rearrange("p (c i) t -> p c t i", i=4), z2_rows[:, :, cols].rearrange("p t (c i) -> p c t i", i=4))
+            nc.vector.quantize_mx(out=z2_codes[:, cols].bitcast(FP8X4), scales=z2_plane[:, cols], in_=half[:].rearrange("p c t -> p (c t)"))
         h_banks = [psum.tile([P, S], F32, name=f"bank_b{t}") for t in range(PACK)]
         with_z = (w2_codes, w23_plane, z_codes, z_plane)
         with_z2 = (w3_codes, w23_plane[4:], z2_codes, z2_plane)

from contextlib import ExitStack

import concourse.mybir as mybir

F32 = mybir.dt.float32
BF16 = mybir.dt.bfloat16
I32 = mybir.dt.int32
U32 = mybir.dt.uint32
U16 = mybir.dt.uint16
U8 = mybir.dt.uint8
FP8X4 = mybir.dt.float8_e4m3fn_x4
COPY = mybir.ActivationFunctionType.Copy
ADD = mybir.AluOpType.add
SUB = mybir.AluOpType.subtract
MULT = mybir.AluOpType.mult
MAX = mybir.AluOpType.max
MIN = mybir.AluOpType.min

P = 128
PACK = 4
S = 512
T = 1024
G = 2048
PAIRS = 256
U = 384
Y_WINDOW = 544
H_WINDOW = 768
V_COLS = 352
FLOPS = 4 * 2 * 512 * 512 * 512


def tile_picked_jkeywindliftkmin_none_po_kernel(
    tc, x_words, x_scales, w1_words, w1_scales, d_words, d_scales, gn, gk, w2_words, w2_scales,
    w3_words, w3_scales, offs, kidx, two, n1, n2, n3, n4, n5, n6, out_0, out_1, out_2
):
    nc = tc.nc
    with ExitStack() as ctx:
        keep = ctx.enter_context(tc.tile_pool(name="keep", bufs=1))
        psum = ctx.enter_context(tc.psum_pool(name="psum", bufs=1))

        def sb(shape, dtype, name):
            return keep.tile(shape, dtype, name=name, align_bytes=64)

        def load_list(src, name):
            dst = keep.tile([P, src.shape[1]], U16, name=name)
            nc.sync.dma_start(dst[:], src)
            return dst

        def load_words(src, name):
            dst = sb([P, src.shape[2]], I32, name)
            nc.sync.dma_start(dst[:], src[0].rearrange("p c r -> p (c r)").bitcast(I32))
            return dst

        def load_scale_rows(queues, dst, src, first):
            for q in range(4):
                queue = queues[q % len(queues)]
                rows = slice(32 * q + first, 32 * q + first + 4)
                queue.dma_start(dst[rows, :].bitcast(I32), src[0, 4 * q : 4 * q + 4, :].bitcast(I32))

        def zeroed_bytes(width, name, engine):
            dst = sb([P, width], U8, name)
            engine.memset(dst[:].bitcast(I32), 0)
            return dst

        def dealt(src, dtype, name, engine=nc.vector):
            dst = sb([P, S], dtype, name)
            engine.tensor_copy(dst[:].rearrange("p (t m) -> p t m", t=PACK), src.rearrange("p (m t) -> p t m", t=PACK))
            return dst

        def picked(table, offsets, dtype, name):
            dst = sb([P, S], dtype, name)
            nc.vector.tensor_copy(dst[:], table.indirect(offsets[:]))
            return dst

        def product(bank, t, w_codes, w_plane, codes, plane, start, stop):
            cols = slice(P * t, P * (t + 1))
            nc.tensor.matmul_mx(out=bank[:], lhsT=w_codes[:, cols].bitcast(FP8X4), lhsT_scale=w_plane[:, cols],
                                rhs=codes[:].bitcast(FP8X4), rhs_scale=plane[:], start=start, stop=stop)

        def interleave(copy, dst, src, cols):
            copy(dst[:, cols, :].rearrange("p (c i) t -> p c t i", i=4), src[:, :, cols].rearrange("p t (c i) -> p c t i", i=4))

        def quantise(grouped, name):
            codes = sb([P, S], U32, name + "_codes")
            plane = sb([P, S], U8, name + "_plane")
            nc.vector.quantize_mx(out=codes[:].bitcast(FP8X4), scales=plane[:], in_=grouped[:].rearrange("p c t -> p (c t)"))
            return codes, plane

        xs = zeroed_bytes(T, "xs", nc.gpsimd)
        w1s = zeroed_bytes(S, "w1s", nc.gpsimd)
        ds = zeroed_bytes(G, "ds", nc.vector)
        w23s = zeroed_bytes(S, "w23s", nc.vector)
        offs_t = load_list(offs, "offs_t")
        xw = load_words(x_words, "xw")
        w1w = load_words(w1_words, "w1w")
        load_scale_rows([nc.scalar, nc.sync], xs, x_scales, 0)
        load_scale_rows([nc.scalar, nc.sync], w1s, w1_scales, 0)
        kidx_t = load_list(kidx, "kidx_t")
        nc.sync.dma_start(ds[0:P:8, :].bitcast(I32), d_scales[0].bitcast(I32))
        two_t = load_list(two, "two_t")
        n1_t = load_list(n1, "n1_t")
        n2_t = load_list(n2, "n2_t")
        dw = load_words(d_words, "dw")
        n3_t = load_list(n3, "n3_t")
        n4_t = load_list(n4, "n4_t")
        w23w = sb([P, 2, S], I32, "w23w")
        for a, src in enumerate((w2_words, w3_words)):
            nc.sync.dma_start(w23w[:, a, :], src[0].rearrange("p c r -> p (c r)").bitcast(I32))

        y = [sb([P, Y_WINDOW], F32, f"y{t}") for t in range(PACK)]
        h = [sb([P, H_WINDOW], F32, f"h{t}") for t in range(PACK)]
        for t in range(PACK):
            nc.gpsimd.memset(y[t][:, S:], 0.0)
        for t in range(PACK):
            nc.gpsimd.memset(h[t][:, S:], 0.0)

        w1_codes = dealt(w1w[:].bitcast(U32), U32, "w1_codes", nc.gpsimd)
        xq_codes = picked(xw[:].bitcast(U32), offs_t, U32, "xq_codes")
        xq_plane = picked(xs[:], offs_t, U8, "xq_plane")
        w1_plane = dealt(w1s[:], U8, "w1_plane")

        def y_product(t, tag):
            bank = psum.tile([P, S], F32, name=tag)
            product(bank, t, w1_codes, w1_plane, xq_codes, xq_plane, True, True)
            return bank

        y_first = [y_product(t, f"bank_b{t}") for t in range(2)]

        key_bytes = dealt(picked(ds[:], kidx_t, U8, "key_bytes_picked")[:], U8, "key_bytes")
        key_plane = sb([P, S], U8, "key_plane")
        for q in range(4):
            nc.sync.dma_start(key_plane[32 * q : 32 * q + 4, :].bitcast(I32), key_bytes[32 * q : 32 * q + 32 : 8, :].bitcast(I32))
        gn_t = sb([P, PACK], F32, "gn_t")
        nc.sync.dma_start(gn_t[:], gn.rearrange("(p t) o -> p (t o)", t=PACK))
        load_scale_rows([nc.sync], w23s, w2_scales, 0)
        load_scale_rows([nc.sync], w23s, w3_scales, 4)
        gk_t = sb([P, PACK], F32, "gk_t")
        nc.sync.dma_start(gk_t[:], gk.rearrange("(p t) o -> p (t o)", t=PACK))
        n5_t = load_list(n5, "n5_t")
        n6_t = load_list(n6, "n6_t")
        xt_plane = picked(xs[:], two_t, U8, "xt_plane")
        xt_codes = picked(xw[:].bitcast(U32), two_t, U32, "xt_codes")
        key_codes = dealt(picked(dw[:].bitcast(U32), kidx_t, U32, "key_codes_picked")[:], U32, "key_codes")
        s_banks = [psum.tile([P, S], F32, name=f"bank_a{t}") for t in range(PACK)]
        for t in range(PACK):
            product(s_banks[t], t, key_codes, key_plane, xt_codes, xt_plane, True, True)

        z_rows = sb([P, PACK, S], BF16, "z_rows")

        def fetch_y(t, bank, at_n1, at_n2):
            nc.scalar.copy(y[t][:, :S], bank[:])
            nc.scalar.activation(at_n1, y[t][:].indirect(n1_t[:]), COPY)
            nc.scalar.activation(at_n2, y[t][:].indirect(n2_t[:]), COPY)

        def scale_z(t, bank, diff):
            nc.vector.scalar_tensor_tensor(z_rows[:, t, :], diff, gn_t[:, t : t + 1], bank[:], MULT, MULT)

        def pair_s(first, tags):
            neg_pa = sb([P, 2, PAIRS], F32, f"neg_pa{first}")
            pb = sb([P, 2, PAIRS], F32, f"pb{first}")
            rb = sb([P, 2, PAIRS], F32, f"rb{first}")
            dt = [sb([P, S], F32, f"dt{first + a}") for a in range(2)]
            for a in range(2):
                s = sb([P, S], F32, tags[a])
                nc.scalar.activation(s[:], s_banks[first + a][:], COPY, scale=0.0625)
                nc.scalar.activation(neg_pa[:, a, :], s[:].indirect(n3_t[:]), COPY, scale=-1.0)
                nc.scalar.activation(pb[:, a, :], s[:].indirect(n4_t[:]), COPY)
                nc.vector.tensor_tensor(dt[a][:].indirect(n3_t[:]), pb[:, a, :], neg_pa[:, a, :], ADD)
            nc.vector.scalar_tensor_tensor(rb[:], neg_pa[:], -0.5, pb[:], MULT, MAX)
            for a in range(2):
                nc.vector.tensor_copy(dt[a][:].indirect(n4_t[:]), rb[:, a, :])
            return dt

        at_n1 = [sb([P, S], F32, f"at_n1{t}") for t in range(2)]
        at_n2 = [sb([P, S], F32, f"at_n2{t}") for t in range(2)]
        fetch_y(0, y_first[0], at_n1[0][:], at_n2[0][:])
        diff0 = sb([P, S], F32, "key_codes_picked")
        nc.vector.tensor_tensor(diff0[:], at_n1[0][:], at_n2[0][:], SUB)
        w23_codes = sb([P, 2, S], I32, "dw")
        nc.vector.tensor_copy(w23_codes[:].rearrange("p a (t m) -> p a t m", t=PACK), w23w[:].rearrange("p a (m t) -> p a t m", t=PACK))
        w2_codes = w23_codes[:, 0, :]
        w3_codes = w23_codes[:, 1, :]
        scale_z(0, y_first[0], diff0[:])
        fetch_y(1, y_first[1], at_n1[1][:], at_n2[1][:])
        diff1 = sb([P, S], F32, "at_n10")
        nc.vector.tensor_tensor(diff1[:], at_n1[1][:], at_n2[1][:], SUB)
        scale_z(1, y_first[1], diff1[:])
        dts = pair_s(0, ["s0", "s1"])

        def late_z(t, bank):
            late_n1 = sb([P, S], F32, f"at_n1{t}")
            late_n2 = sb([P, S], F32, f"at_n2{t}")
            fetch_y(t, bank, late_n1[:], late_n2[:])
            diff = sb([P, S], F32, f"diff{t}")
            nc.gpsimd.tensor_tensor(diff[:], late_n1[:], late_n2[:], SUB)
            scale_z(t, bank, diff[:])

        def fetch_s(t, tag):
            s = sb([P, S], F32, tag)
            neg_pa = sb([P, PAIRS], F32, f"neg_pa{t}")
            pb = sb([P, PAIRS], F32, f"pb{t}")
            dt = sb([P, S], F32, f"dt{t}")
            nc.scalar.activation(s[:], s_banks[t][:], COPY, scale=0.0625)
            nc.scalar.activation(neg_pa[:], s[:].indirect(n3_t[:]), COPY, scale=-1.0)
            nc.scalar.activation(pb[:], s[:].indirect(n4_t[:]), COPY)
            rb = sb([P, PAIRS], F32, f"rb{t}")
            nc.vector.scalar_tensor_tensor(rb[:], neg_pa[:], -0.5, pb[:], MULT, MAX)
            nc.vector.tensor_tensor(dt[:].indirect(n3_t[:]), pb[:], neg_pa[:], ADD)
            nc.vector.tensor_copy(dt[:].indirect(n4_t[:]), rb[:])
            return dt

        w23_plane = dealt(w23s[:], U8, "pb0")
        late_z(2, y_product(2, "bank_a1"))
        dts.append(fetch_s(2, "y2"))
        late_z(3, y_product(3, "bank_a2"))
        dts.append(fetch_s(3, "y3"))

        z2_rows = sb([P, PACK, S], BF16, "y3")
        for t in range(2):
            nc.scalar.activation(z2_rows[:, t, :], dts[t][:], COPY, scale=gk_t[:, t : t + 1])
        z_grouped = sb([P, S, PACK], BF16, "z_grouped")
        interleave(nc.scalar.copy, z_grouped, z_rows, slice(0, S))
        nc.scalar.activation(z2_rows[:, 2, :], dts[2][:], COPY, scale=gk_t[:, 2:3])
        nc.vector.tensor_scalar(z2_rows[:, 3, :], dts[3][:], gk_t[:, 3:4], None, MULT)
        z_codes, z_plane = quantise(z_grouped, "z")
        z2_codes = sb([P, S], U32, "z2_codes")
        z2_plane = sb([P, S], U8, "z2_plane")
        for copy, cols, tag in ((nc.vector.tensor_copy, slice(0, S // 2), "z_grouped"), (nc.scalar.copy, slice(S // 2, S), "z2_grouped")):
            half = sb([P, S // 2, PACK], BF16, tag)
            copy(half[:].rearrange("p (c i) t -> p c t i", i=4), z2_rows[:, :, cols].rearrange("p t (c i) -> p c t i", i=4))
            nc.vector.quantize_mx(out=z2_codes[:, cols].bitcast(FP8X4), scales=z2_plane[:, cols], in_=half[:].rearrange("p c t -> p (c t)"))
        h_banks = [psum.tile([P, S], F32, name=f"bank_b{t}") for t in range(PACK)]
        with_z = (w2_codes, w23_plane, z_codes, z_plane)
        with_z2 = (w3_codes, w23_plane[4:], z2_codes, z2_plane)
        for t in range(2):
            product(h_banks[t], t, *with_z, True, False)
        for t in range(2):
            product(h_banks[t], t, *with_z2, False, True)
        for t in range(2, PACK):
            product(h_banks[t], t, *with_z2, True, False)
            product(h_banks[t], t, *with_z, False, True)

        out_rows = out_0.rearrange("(p t) j -> p t j", t=PACK)
        o_rows = sb([P, PACK, S], BF16, "o_rows")
        neg_half = [sb([P, U], F32, f"neg_half{t}") for t in range(PACK)]
        old = [sb([P, U], F32, f"old{t}") for t in range(PACK)]
        least = [sb([P, U], F32, f"least{t}") for t in range(PACK)]

        def fetch_on_scalar(t):
            nc.scalar.copy(h[t][:, :S], h_banks[t][:])
            nc.scalar.activation(neg_half[t][:], h[t][:].indirect(n6_t[:]), COPY, scale=-0.5)
            nc.scalar.activation(old[t][:], h[t][:].indirect(n5_t[:]), COPY)

        def take_least(t):
            nc.vector.scalar_tensor_tensor(least[t][:], neg_half[t][:], -2.0, old[t][:], MULT, MIN)

        def put_on_vector(t):
            nc.vector.tensor_tensor(h[t][:].indirect(n5_t[:]), least[t][:], neg_half[t][:], ADD)

        def sum_for_scalar(t):
            nc.vector.tensor_tensor(old[t][:], least[t][:], neg_half[t][:], ADD)

        def put_on_scalar(t):
            nc.scalar.activation(h[t][:].indirect(n5_t[:]), old[t][:], COPY)

        def finish(t):
            nc.sync.dma_start(out_rows[:, t, :], h[t][:, :S])
            nc.vector.tensor_copy(o_rows[:, t, :], h[t][:, :S])

        pa2 = sb([P, U], F32, "pa2")
        nc.vector.tensor_copy(h[0][:, :S], h_banks[0][:])
        nc.vector.tensor_copy(pa2[:], h[0][:].indirect(n6_t[:]))
        nc.vector.tensor_copy(old[0][:], h[0][:].indirect(n5_t[:]))
        nc.vector.tensor_scalar(neg_half[0][:], pa2[:], -0.5, None, MULT)
        nc.vector.tensor_tensor(least[0][:], pa2[:], old[0][:], MIN)
        fetch_on_scalar(1)
        fetch_on_scalar(2)
        fetch_on_scalar(3)
        put_on_vector(0)
        take_least(1)
        sum_for_scalar(1)
        finish(0)
        take_least(2)
        sum_for_scalar(2)
        put_on_scalar(1)
        take_least(3)
        put_on_vector(3)
        put_on_scalar(2)
        finish(1)
        finish(3)
        finish(2)

        o_grouped = sb([P, S, PACK], BF16, "o_grouped")
        interleave(nc.vector.tensor_copy, o_grouped, o_rows, slice(0, V_COLS))
        interleave(nc.scalar.copy, o_grouped, o_rows, slice(V_COLS, S))
        o_codes, o_plane = quantise(o_grouped, "o")
        nc.sync.dma_start(out_1[0].rearrange("p c r -> p (c r)").bitcast(I32), o_codes[:].bitcast(I32))
        for q in range(4):
            queue = nc.scalar if q % 2 == 0 else nc.sync
            queue.dma_start(out_2[0, 4 * q : 4 * q + 4, :].bitcast(I32), o_plane[32 * q : 32 * q + 4, :].bitcast(I32))
